import numpy as np
import ml_dtypes


def mxq(x, axis, fmt="e4m3"):
    dtype, down = {"e4m3": (ml_dtypes.float8_e4m3fn, 7), "e5m2": (ml_dtypes.float8_e5m2, 14)}[fmt]
    v = np.moveaxis(np.asarray(x, np.float32).astype(ml_dtypes.bfloat16).astype(np.float64), axis, -1)
    blocks = v.reshape(v.shape[:-1] + (-1, 32))
    amax = np.abs(blocks).max(-1, keepdims=True)
    byte = np.maximum(np.where(amax > 0, np.frexp(amax)[1] - 1 + 127, 0) - down, 1)
    scale = np.exp2(byte - 127.0)
    codes = (blocks / scale).astype(np.float32).astype(dtype).astype(np.float64)
    return np.moveaxis((codes * scale).reshape(v.shape), -1, axis)


WIDE = False


def mx_kscale(k, group=512):
    if not WIDE:
        return np.ones(k)
    levels = np.array([18, -18])
    if group != 512:
        return np.exp2(np.random.permutation(np.resize(levels, k // group))).repeat(group)
    if k % 512:
        return np.exp2(np.random.permutation(np.resize(levels, k // 32))).repeat(32)
    a = np.empty((k // 512, 16))
    for p in range(k // 512):
        a[p, :8] = np.random.permutation(np.resize(levels, 8))
        for g in range(8):
            far = levels[np.abs(levels - a[p, g]) >= 10]
            a[p, g + 8] = far[np.random.randint(len(far))]
    return np.exp2(a.ravel()).repeat(32)


def f64(x):
    return np.asarray(x).astype(np.float64)


G, D, M, N = 4, 128, 128, 512


def setup_inputs():
    n = np.random.standard_normal
    s_d = mx_kscale(D, 0)
    return {
        "x": (n((G, D, N)) * s_d[:, None]).astype(np.float32),
        "fc": (np.cos(2 * np.pi * np.outer(np.arange(D), np.arange(M)) / D) * (2 / np.sqrt(D)) / s_d[:, None]).astype(np.float32),
        "fs": (np.sin(2 * np.pi * (np.outer(np.arange(D), np.arange(M)) + 0.25) / D) * (2 / np.sqrt(D)) / s_d[:, None]).astype(np.float32),
    }


def reference(x, fc, fs):
    fcq = mxq(f64(fc), 0, "e4m3")
    xq = mxq(f64(x), 1, "e4m3")
    re = fcq.T @ xq
    fsq = mxq(f64(fs), 0, "e4m3")
    im = fsq.T @ xq
    y = 0.5 * np.log(np.square(re) + np.square(im) + 0.001)
    return y

@@ -1,0 +1,183 @@
+from contextlib import ExitStack
+
+import concourse.mybir as mybir
+
+G, D, M, N = 4, 128, 128, 512
+FLOPS = 2 * 2 * G * D * M * N
+
+F32 = mybir.dt.float32
+BF16 = mybir.dt.bfloat16
+I32 = mybir.dt.int32
+U32 = mybir.dt.uint32
+U8 = mybir.dt.uint8
+FP8X4 = mybir.dt.float8_e4m3fn_x4
+ACT = mybir.ActivationFunctionType
+ALU = mybir.AluOpType
+
+P = 128
+PACK = 4
+ROWS = D // PACK
+W = 128
+CHUNKS = N // W
+SLOTS = [[[0, 0], [0, 1]], [[1, 0], [1, 1]], [[0, 2], [0, 3]], [[1, 2], [1, 3]]]
+
+
+def tile_rows_dft_logmag_kernel(tc, x, fc, fs, out):
+    nc = tc.nc
+    x_rows = x.rearrange("g (p j) n -> (g p) j n", j=PACK)
+    out_rows = out.rearrange("g m n -> m g n")
+    fc_rows = fc.rearrange("(p j) m -> p j m", j=PACK)
+    fs_rows = fs.rearrange("(p j) m -> p j m", j=PACK)
+
+    with ExitStack() as ctx:
+        sb = ctx.enter_context(tc.tile_pool(name="sb", bufs=1))
+        ps = ctx.enter_context(tc.psum_pool(name="ps", bufs=1))
+        ctx.enter_context(tc.manual_schedule())
+
+        warm = sb.tile([P, 2], F32, name="warm")
+        f_raw = sb.tile([P, PACK, M], F32, name="f_raw")
+        f_bf = sb.tile([P, M, PACK], BF16, name="f_bf", align_bytes=64)
+        f_mx = [sb.tile([P, M + M // 4], U32, name="f_mx%d" % s, align_bytes=64) for s in range(2)]
+        x_raw = {}
+        x_bf = sb.tile([P, N, PACK], BF16, name="x_bf", align_bytes=64)
+        x_codes = sb.tile([P, N], U32, name="x_codes", align_bytes=64)
+        x_scales = sb.tile([P, N], U8, name="x_scales", align_bytes=64)
+        sums = sb.tile([P, CHUNKS, G, 2, W], F32, name="sums")
+        squares = sb.tile([P, CHUNKS, G, 2, W], F32, name="squares")
+        power = sb.tile([P, CHUNKS, G, W], F32, name="power")
+        logp = sb.tile([P, CHUNKS, G, W], F32, name="logp")
+        result = sb.tile([P, CHUNKS, G, W], F32, name="result")
+        acc = [[ps.tile([P, 4, W], F32, name="acc%d_%d" % (g, b)) for b in range(2)] for g in range(G)]
+
+        def rows(g):
+            return slice(ROWS * g, ROWS * (g + 1))
+
+        def cols(cs):
+            return slice(W * cs[0], W * (cs[-1] + 1))
+
+        def span(v):
+            return slice(min(v), max(v) + 1)
+
+        def load_basis(g, queue):
+            queue.dma_start(out=f_raw[rows(g), :, :], in_=fc_rows if g < G // 2 else fs_rows)
+
+        def load_x(cs):
+            raw = sb.tile([P, PACK, W * len(cs)], F32, name="x_raw%d" % cs[0])
+            for i, c in enumerate(cs):
+                x_raw[c] = (raw, i)
+            nc.sync.dma_start(out=raw[:], in_=x_rows[:, :, cols(cs)])
+
+        def interleave(dst, src):
+            nc.vector.tensor_copy(out=dst, in_=src.rearrange("p j w -> p w j"))
+
+        def quantize(codes, scales, src):
+            nc.vector.quantize_mx(out=codes.bitcast(FP8X4), scales=scales, in_=src.rearrange("p w j -> p (w j)"))
+
+        def interleave_x(cs):
+            raw, i = x_raw[cs[0]]
+            interleave(x_bf[:, cols(cs), :], raw[:, :, W * i : W * (i + len(cs))])
+
+        def quantize_x(cs):
+            quantize(x_codes[:, cols(cs)], x_scales[:, cols(cs)], x_bf[:, cols(cs), :])
+
+        def swap_halves():
+            half = P // 2
+            nc.scalar.dma_start(out=f_mx[1][half:, :].bitcast(I32), in_=f_mx[0][:half, :].bitcast(I32))
+            nc.scalar.dma_start(out=f_mx[1][:half, :].bitcast(I32), in_=f_mx[0][half:, :].bitcast(I32))
+
+        def multiply(c, order):
+            for s, g in order:
+                bank, place = SLOTS[c][s]
+                nc.tensor.matmul_mx(
+                    out=acc[g][bank][:, place, :],
+                    lhsT=f_mx[s][rows(g), :M].bitcast(FP8X4),
+                    lhsT_scale=f_mx[s][rows(g), M:].bitcast(U8),
+                    rhs=x_codes[rows(g), cols([c])].bitcast(FP8X4),
+                    rhs_scale=x_scales[rows(g), cols([c])],
+                    start=True, stop=True)
+
+        def products(c, ss, g):
+            bank, place = SLOTS[c][ss[0]]
+            return acc[g][bank][:, place : place + len(ss), :]
+
+        def square(c, ss, gs):
+            for g in gs:
+                nc.scalar.activation(out=squares[:, c, g, span(ss), :], in_=products(c, ss, g), func=ACT.Square)
+
+        def copy_out(c, ss, g):
+            nc.vector.tensor_copy(out=sums[:, c, g, span(ss), :], in_=products(c, ss, g))
+
+        def square_copy(c, ss, g):
+            nc.vector.tensor_tensor(out=squares[:, c, g, span(ss), :], in0=sums[:, c, g, span(ss), :],
+                                    in1=sums[:, c, g, span(ss), :], op=ALU.mult)
+
+        def add(c, gs):
+            nc.vector.scalar_tensor_tensor(out=power[:, c, span(gs), :], in0=squares[:, c, span(gs), 0, :],
+                                           scalar=0.001, in1=squares[:, c, span(gs), 1, :],
+                                           op0=ALU.add, op1=ALU.add)
+
+        def log(c, gs):
+            nc.scalar.activation(out=logp[:, c, span(gs), :], in_=power[:, c, span(gs), :], func=ACT.Ln)
+
+        def halve(c, gs):
+            nc.vector.tensor_scalar(out=result[:, c, span(gs), :], in0=logp[:, c, span(gs), :], scalar1=0.5,
+                                    scalar2=None, op0=ALU.mult)
+
+        def store(c, gs, queue):
+            queue.dma_start(out=out_rows[:, span(gs), cols([c])], in_=result[:, c, span(gs), :])
+
+        load_basis(0, nc.sync)
+        load_basis(2, nc.scalar)
+        load_basis(1, nc.sync)
+        load_basis(3, nc.scalar)
+        load_x([0])
+        nc.vector.memset(warm[:, 0:1], 1.0)
+        nc.vector.memset(f_mx[0][:, M:], 0)
+        nc.scalar.activation(out=warm[:, 1:2], in_=warm[:, 0:1], func=ACT.Ln)
+        load_x([1])
+        load_x([2, 3])
+        interleave(f_bf[:], f_raw[:])
+        quantize(f_mx[0][:, :M], f_mx[0][:, M:].bitcast(U8), f_bf[:])
+        swap_halves()
+        interleave_x([0])
+        quantize_x([0])
+        multiply(0, [[0, 0], [0, 1], [0, 2], [0, 3]])
+        square(0, [0], [0, 1, 2, 3])
+        interleave_x([1])
+        quantize_x([1])
+        multiply(1, [[0, 0], [0, 1], [0, 2], [0, 3]])
+        square(1, [0], [0, 1, 2, 3])
+        multiply(0, [[1, 0], [1, 1], [1, 2], [1, 3]])
+        square(0, [1], [0, 1, 2, 3])
+        multiply(1, [[1, 0], [1, 1], [1, 2], [1, 3]])
+        square(1, [1], [0, 1, 2, 3])
+        interleave_x([2, 3])
+        quantize_x([2, 3])
+        multiply(2, [[0, 3], [0, 2], [1, 3], [0, 1], [1, 2], [0, 0], [1, 1], [1, 0]])
+        add(0, [0, 1, 2, 3])
+        log(0, [0, 1, 2, 3])
+        add(1, [0, 1, 2, 3])
+        multiply(3, [[0, 3], [0, 2], [1, 3], [0, 1], [1, 2], [0, 0], [1, 1], [1, 0]])
+        square(2, [0, 1], [2, 1, 0])
+        copy_out(2, [0, 1], 3)
+        halve(0, [0, 1, 2, 3])
+        store(0, [0, 1, 2, 3], nc.sync)
+        square_copy(2, [0, 1], 3)
+        log(1, [0, 1, 2, 3])
+        copy_out(3, [0, 1], 3)
+        add(2, [0, 1, 2, 3])
+        square_copy(3, [0, 1], 3)
+        halve(1, [0, 1, 2, 3])
+        store(1, [0, 1, 2, 3], nc.sync)
+        square(3, [0, 1], [2, 1, 0])
+        log(2, [0, 1, 2, 3])
+        add(3, [2, 3])
+        add(3, [0, 1])
+        halve(2, [0, 1, 2, 3])
+        store(2, [0, 1, 2, 3], nc.sync)
+        log(3, [2, 3])
+        halve(3, [2, 3])
+        store(3, [2, 3], nc.sync)
+        log(3, [0, 1])
+        halve(3, [0, 1])
+        store(3, [0, 1], nc.sync)

@@ -18,8 +18,6 @@ P = 128
 PACK = 4
 ROWS = D // PACK
 W = 128
-CHUNKS = N // W
-SLOTS = [[[0, 0], [0, 1]], [[1, 0], [1, 1]], [[0, 2], [0, 3]], [[1, 2], [1, 3]]]
 
 
 def tile_rows_dft_logmag_kernel(tc, x, fc, fs, out):
@@ -42,142 +40,190 @@ def tile_rows_dft_logmag_kernel(tc, x, fc, fs, out):
         x_bf = sb.tile([P, N, PACK], BF16, name="x_bf", align_bytes=64)
         x_codes = sb.tile([P, N], U32, name="x_codes", align_bytes=64)
         x_scales = sb.tile([P, N], U8, name="x_scales", align_bytes=64)
-        sums = sb.tile([P, CHUNKS, G, 2, W], F32, name="sums")
-        squares = sb.tile([P, CHUNKS, G, 2, W], F32, name="squares")
-        power = sb.tile([P, CHUNKS, G, W], F32, name="power")
-        logp = sb.tile([P, CHUNKS, G, W], F32, name="logp")
-        result = sb.tile([P, CHUNKS, G, W], F32, name="result")
+        sums = sb.tile([P, G, 2, 4, W], F32, name="sums")
+        squares = sb.tile([P, G, 2, 4, W], F32, name="squares")
+        power = sb.tile([P, G, N], F32, name="power")
+        logp = sb.tile([P, G, N], F32, name="logp")
+        result = sb.tile([P, G, N], F32, name="result")
         acc = [[ps.tile([P, 4, W], F32, name="acc%d_%d" % (g, b)) for b in range(2)] for g in range(G)]
 
         def rows(g):
             return slice(ROWS * g, ROWS * (g + 1))
 
-        def cols(cs):
-            return slice(W * cs[0], W * (cs[-1] + 1))
-
-        def span(v):
-            return slice(min(v), max(v) + 1)
+        def cols(c0, c1):
+            return slice(W * c0, W * c1)
 
         def load_basis(g, queue):
             queue.dma_start(out=f_raw[rows(g), :, :], in_=fc_rows if g < G // 2 else fs_rows)
 
-        def load_x(cs):
-            raw = sb.tile([P, PACK, W * len(cs)], F32, name="x_raw%d" % cs[0])
-            for i, c in enumerate(cs):
-                x_raw[c] = (raw, i)
-            nc.sync.dma_start(out=raw[:], in_=x_rows[:, :, cols(cs)])
+        def load_x(c0, c1):
+            raw = sb.tile([P, PACK, W * (c1 - c0)], F32, name="x_raw%d" % c0)
+            for c in range(c0, c1):
+                x_raw[c] = (raw, c0)
+            nc.sync.dma_start(out=raw[:], in_=x_rows[:, :, cols(c0, c1)])
 
         def interleave(dst, src):
-            nc.vector.tensor_copy(out=dst, in_=src.rearrange("p j w -> p w j"))
+            nc.vector.tensor_copy(out=dst.rearrange("p (c i) j -> p c j i", i=4),
+                                  in_=src.rearrange("p j (c i) -> p c j i", i=4))
 
         def quantize(codes, scales, src):
             nc.vector.quantize_mx(out=codes.bitcast(FP8X4), scales=scales, in_=src.rearrange("p w j -> p (w j)"))
 
-        def interleave_x(cs):
-            raw, i = x_raw[cs[0]]
-            interleave(x_bf[:, cols(cs), :], raw[:, :, W * i : W * (i + len(cs))])
+        def interleave_x(c0, c1):
+            raw, first = x_raw[c0]
+            interleave(x_bf[:, cols(c0, c1), :], raw[:, :, cols(c0 - first, c1 - first)])
 
-        def quantize_x(cs):
-            quantize(x_codes[:, cols(cs)], x_scales[:, cols(cs)], x_bf[:, cols(cs), :])
+        def quantize_x(c0, c1):
+            quantize(x_codes[:, cols(c0, c1)], x_scales[:, cols(c0, c1)], x_bf[:, cols(c0, c1), :])
 
         def swap_halves():
             half = P // 2
             nc.scalar.dma_start(out=f_mx[1][half:, :].bitcast(I32), in_=f_mx[0][:half, :].bitcast(I32))
             nc.scalar.dma_start(out=f_mx[1][:half, :].bitcast(I32), in_=f_mx[0][half:, :].bitcast(I32))
 
-        def multiply(c, order):
-            for s, g in order:
-                bank, place = SLOTS[c][s]
+        def multiply(*passes):
+            for c, s, g in passes:
                 nc.tensor.matmul_mx(
-                    out=acc[g][bank][:, place, :],
+                    out=acc[g][c % 2][:, 2 * (c // 2) + s, :],
                     lhsT=f_mx[s][rows(g), :M].bitcast(FP8X4),
                     lhsT_scale=f_mx[s][rows(g), M:].bitcast(U8),
-                    rhs=x_codes[rows(g), cols([c])].bitcast(FP8X4),
-                    rhs_scale=x_scales[rows(g), cols([c])],
+                    rhs=x_codes[rows(g), cols(c, c + 1)].bitcast(FP8X4),
+                    rhs_scale=x_scales[rows(g), cols(c, c + 1)],
                     start=True, stop=True)
 
-        def products(c, ss, g):
-            bank, place = SLOTS[c][ss[0]]
-            return acc[g][bank][:, place : place + len(ss), :]
+        def square(g, b, lo, hi):
+            nc.scalar.activation(out=squares[:, g, b, lo:hi, :], in_=acc[g][b][:, lo:hi, :], func=ACT.Square)
 
-        def square(c, ss, gs):
-            for g in gs:
-                nc.scalar.activation(out=squares[:, c, g, span(ss), :], in_=products(c, ss, g), func=ACT.Square)
+        def copy_out(g, b, lo, hi):
+            nc.vector.tensor_copy(out=sums[:, g, b, lo:hi, :], in_=acc[g][b][:, lo:hi, :])
 
-        def copy_out(c, ss, g):
-            nc.vector.tensor_copy(out=sums[:, c, g, span(ss), :], in_=products(c, ss, g))
+        def square_copy(g, b, lo, hi):
+            nc.vector.tensor_tensor(out=squares[:, g, b, lo:hi, :], in0=sums[:, g, b, lo:hi, :],
+                                    in1=sums[:, g, b, lo:hi, :], op=ALU.mult)
 
-        def square_copy(c, ss, g):
-            nc.vector.tensor_tensor(out=squares[:, c, g, span(ss), :], in0=sums[:, c, g, span(ss), :],
-                                    in1=sums[:, c, g, span(ss), :], op=ALU.mult)
+        def add(c0, c1, g0, g1):
+            banks = slice(c0 % 2, c0 % 2 + c1 - c0)
+            place = 2 * (c0 // 2)
+            nc.vector.scalar_tensor_tensor(
+                out=power[:, g0:g1, cols(c0, c1)].rearrange("p g (c w) -> p g c w", w=W),
+                in0=squares[:, g0:g1, banks, place, :], scalar=0.001, in1=squares[:, g0:g1, banks, place + 1, :],
+                op0=ALU.add, op1=ALU.add)
 
-        def add(c, gs):
-            nc.vector.scalar_tensor_tensor(out=power[:, c, span(gs), :], in0=squares[:, c, span(gs), 0, :],
-                                           scalar=0.001, in1=squares[:, c, span(gs), 1, :],
-                                           op0=ALU.add, op1=ALU.add)
+        def log(c0, c1, g0, g1):
+            nc.scalar.activation(out=logp[:, g0:g1, cols(c0, c1)], in_=power[:, g0:g1, cols(c0, c1)], func=ACT.Ln)
 
-        def log(c, gs):
-            nc.scalar.activation(out=logp[:, c, span(gs), :], in_=power[:, c, span(gs), :], func=ACT.Ln)
+        def halve(c0, c1, g0, g1):
+            nc.vector.tensor_scalar(out=result[:, g0:g1, cols(c0, c1)], in0=logp[:, g0:g1, cols(c0, c1)],
+                                    scalar1=0.5, scalar2=None, op0=ALU.mult)
 
-        def halve(c, gs):
-            nc.vector.tensor_scalar(out=result[:, c, span(gs), :], in0=logp[:, c, span(gs), :], scalar1=0.5,
-                                    scalar2=None, op0=ALU.mult)
+        def halve_scalar(c0, c1, g0, g1):
+            nc.scalar.activation(out=result[:, g0:g1, cols(c0, c1)], in_=logp[:, g0:g1, cols(c0, c1)],
+                                 func=ACT.Copy, scale=0.5)
 
-        def store(c, gs, queue):
-            queue.dma_start(out=out_rows[:, span(gs), cols([c])], in_=result[:, c, span(gs), :])
+        def store(c0, c1, g0, g1):
+            nc.sync.dma_start(out=out_rows[:, g0:g1, cols(c0, c1)], in_=result[:, g0:g1, cols(c0, c1)])
 
         load_basis(0, nc.sync)
         load_basis(2, nc.scalar)
         load_basis(1, nc.sync)
         load_basis(3, nc.scalar)
-        load_x([0])
+        load_x(0, 1)
         nc.vector.memset(warm[:, 0:1], 1.0)
         nc.vector.memset(f_mx[0][:, M:], 0)
         nc.scalar.activation(out=warm[:, 1:2], in_=warm[:, 0:1], func=ACT.Ln)
-        load_x([1])
-        load_x([2, 3])
+        load_x(1, 2)
+        load_x(2, 4)
         interleave(f_bf[:], f_raw[:])
         quantize(f_mx[0][:, :M], f_mx[0][:, M:].bitcast(U8), f_bf[:])
         swap_halves()
-        interleave_x([0])
-        quantize_x([0])
-        multiply(0, [[0, 0], [0, 1], [0, 2], [0, 3]])
-        square(0, [0], [0, 1, 2, 3])
-        interleave_x([1])
-        quantize_x([1])
-        multiply(1, [[0, 0], [0, 1], [0, 2], [0, 3]])
-        square(1, [0], [0, 1, 2, 3])
-        multiply(0, [[1, 0], [1, 1], [1, 2], [1, 3]])
-        square(0, [1], [0, 1, 2, 3])
-        multiply(1, [[1, 0], [1, 1], [1, 2], [1, 3]])
-        square(1, [1], [0, 1, 2, 3])
-        interleave_x([2, 3])
-        quantize_x([2, 3])
-        multiply(2, [[0, 3], [0, 2], [1, 3], [0, 1], [1, 2], [0, 0], [1, 1], [1, 0]])
-        add(0, [0, 1, 2, 3])
-        log(0, [0, 1, 2, 3])
-        add(1, [0, 1, 2, 3])
-        multiply(3, [[0, 3], [0, 2], [1, 3], [0, 1], [1, 2], [0, 0], [1, 1], [1, 0]])
-        square(2, [0, 1], [2, 1, 0])
-        copy_out(2, [0, 1], 3)
-        halve(0, [0, 1, 2, 3])
-        store(0, [0, 1, 2, 3], nc.sync)
-        square_copy(2, [0, 1], 3)
-        log(1, [0, 1, 2, 3])
-        copy_out(3, [0, 1], 3)
-        add(2, [0, 1, 2, 3])
-        square_copy(3, [0, 1], 3)
-        halve(1, [0, 1, 2, 3])
-        store(1, [0, 1, 2, 3], nc.sync)
-        square(3, [0, 1], [2, 1, 0])
-        log(2, [0, 1, 2, 3])
-        add(3, [2, 3])
-        add(3, [0, 1])
-        halve(2, [0, 1, 2, 3])
-        store(2, [0, 1, 2, 3], nc.sync)
-        log(3, [2, 3])
-        halve(3, [2, 3])
-        store(3, [2, 3], nc.sync)
-        log(3, [0, 1])
-        halve(3, [0, 1])
-        store(3, [0, 1], nc.sync)
+        interleave_x(0, 1)
+        quantize_x(0, 1)
+        multiply((0, 0, 0), (0, 0, 1), (0, 0, 2), (0, 0, 3))
+        interleave_x(1, 2)
+        square(1, 0, 0, 1)
+        quantize_x(1, 2)
+        multiply((1, 0, 0), (1, 0, 1))
+        square(2, 0, 0, 1)
+        interleave_x(2, 3)
+        multiply((1, 0, 2))
+        interleave_x(3, 4)
+        multiply((1, 0, 3))
+        square(3, 0, 0, 1)
+        multiply((0, 1, 1))
+        square(0, 0, 0, 1)
+        multiply((1, 1, 2))
+        quantize_x(2, 3)
+        multiply((1, 1, 3), (0, 1, 2))
+        quantize_x(3, 4)
+        square(1, 1, 0, 1)
+        multiply((0, 1, 3))
+        square(0, 1, 0, 1)
+        multiply((0, 1, 0))
+        square(1, 0, 1, 2)
+        square(2, 1, 0, 2)
+        square(2, 0, 1, 2)
+        square(3, 0, 1, 2)
+        multiply((1, 1, 1), (1, 1, 0))
+        copy_out(3, 1, 0, 2)
+        multiply((2, 0, 0), (2, 0, 1), (2, 1, 1))
+        square(1, 1, 1, 2)
+        add(0, 1, 1, 2)
+        square(0, 1, 1, 2)
+        multiply((2, 0, 2), (3, 0, 3), (2, 0, 3), (3, 1, 0))
+        add(0, 1, 2, 4)
+        square_copy(3, 1, 0, 2)
+        square(0, 0, 1, 3)
+        square(1, 0, 2, 4)
+        log(0, 1, 1, 4)
+        square(2, 0, 2, 3)
+        multiply((3, 1, 2))
+        add(0, 1, 0, 1)
+        copy_out(3, 1, 2, 3)
+        add(1, 2, 0, 4)
+        log(0, 1, 0, 1)
+        add(2, 3, 1, 2)
+        multiply((2, 1, 0))
+        halve(0, 1, 0, 4)
+        square(0, 0, 3, 4)
+        multiply((3, 0, 0), (3, 0, 2), (3, 1, 1))
+        square_copy(3, 1, 2, 3)
+        square(0, 1, 2, 4)
+        store(0, 1, 0, 4)
+        log(1, 2, 0, 4)
+        multiply((2, 1, 2), (3, 0, 1))
+        add(2, 4, 0, 1)
+        multiply((2, 1, 3))
+        copy_out(2, 0, 3, 4)
+        halve(1, 2, 0, 4)
+        store(1, 2, 0, 4)
+        square(3, 0, 2, 4)
+        square_copy(2, 0, 3, 4)
+        multiply((3, 1, 3))
+        square(3, 1, 3, 4)
+        log(2, 3, 0, 2)
+        add(2, 4, 3, 4)
+        log(3, 4, 0, 1)
+        square(1, 1, 2, 4)
+        halve(2, 3, 1, 2)
+        add(2, 3, 2, 3)
+        halve(2, 4, 0, 1)
+        square(2, 1, 2, 4)
+        store(2, 3, 1, 2)
+        store(2, 4, 0, 1)
+        log(3, 4, 3, 4)
+        log(2, 3, 3, 4)
+        add(3, 4, 1, 2)
+        log(2, 3, 2, 3)
+        log(3, 4, 1, 2)
+        add(3, 4, 2, 3)
+        halve(3, 4, 3, 4)
+        log(3, 4, 2, 3)
+        halve(2, 3, 3, 4)
+        store(3, 4, 3, 4)
+        store(2, 3, 3, 4)
+        halve(2, 3, 2, 3)
+        store(2, 3, 2, 3)
+        halve(3, 4, 1, 2)
+        halve(3, 4, 2, 3)
+        store(3, 4, 1, 2)
+        store(3, 4, 2, 3)

@@ -18,6 +18,7 @@ P = 128
 PACK = 4
 ROWS = D // PACK
 W = 128
+SPLIT = 80
 
 
 def tile_rows_dft_logmag_kernel(tc, x, fc, fs, out):
@@ -65,6 +66,9 @@ def tile_rows_dft_logmag_kernel(tc, x, fc, fs, out):
         def interleave(dst, src):
             nc.vector.tensor_copy(out=dst.rearrange("p (c i) j -> p c j i", i=4),
                                   in_=src.rearrange("p j (c i) -> p c j i", i=4))
+
+        def interleave_scalar(dst, src):
+            nc.scalar.copy(out=dst, in_=src.rearrange("p j w -> p w j"))
 
         def quantize(codes, scales, src):
             nc.vector.quantize_mx(out=codes.bitcast(FP8X4), scales=scales, in_=src.rearrange("p w j -> p (w j)"))
@@ -133,97 +137,105 @@ def tile_rows_dft_logmag_kernel(tc, x, fc, fs, out):
         nc.scalar.activation(out=warm[:, 1:2], in_=warm[:, 0:1], func=ACT.Ln)
         load_x(1, 2)
         load_x(2, 4)
-        interleave(f_bf[:], f_raw[:])
+        interleave(f_bf[:, :SPLIT, :], f_raw[:, :, :SPLIT])
+        interleave_scalar(f_bf[:, SPLIT:, :], f_raw[:, :, SPLIT:])
+        interleave_scalar(x_bf[:, W * 0 + SPLIT : W * 1, :], x_raw[0][0][:, :, SPLIT:])
         quantize(f_mx[0][:, :M], f_mx[0][:, M:].bitcast(U8), f_bf[:])
         swap_halves()
-        interleave_x(0, 1)
+        interleave(x_bf[:, W * 0 : W * 0 + SPLIT, :], x_raw[0][0][:, :, :SPLIT])
         quantize_x(0, 1)
-        multiply((0, 0, 0), (0, 0, 1), (0, 0, 2), (0, 0, 3))
-        interleave_x(1, 2)
-        square(1, 0, 0, 1)
-        quantize_x(1, 2)
-        multiply((1, 0, 0), (1, 0, 1))
+        interleave_scalar(x_bf[:, W * 1 + SPLIT : W * 2, :], x_raw[1][0][:, :, SPLIT:])
+        multiply((0, 0, 2))
+        interleave(x_bf[:, W * 1 : W * 1 + SPLIT, :], x_raw[1][0][:, :, :SPLIT])
+        multiply((0, 0, 0))
         square(2, 0, 0, 1)
-        interleave_x(2, 3)
-        multiply((1, 0, 2))
-        interleave_x(3, 4)
-        multiply((1, 0, 3))
-        square(3, 0, 0, 1)
-        multiply((0, 1, 1))
+        multiply((0, 0, 1))
+        quantize_x(1, 2)
         square(0, 0, 0, 1)
-        multiply((1, 1, 2))
+        multiply((0, 0, 3))
+        interleave_x(2, 3)
+        interleave_x(3, 4)
+        multiply((1, 0, 2), (1, 0, 3), (1, 0, 1))
         quantize_x(2, 3)
-        multiply((1, 1, 3), (0, 1, 2))
-        quantize_x(3, 4)
+        multiply((1, 0, 0))
+        square(1, 0, 0, 1)
+        multiply((0, 1, 0), (0, 1, 1))
+        square(3, 0, 0, 1)
+        square(2, 1, 0, 1)
+        multiply((1, 1, 3))
         square(1, 1, 0, 1)
-        multiply((0, 1, 3))
-        square(0, 1, 0, 1)
-        multiply((0, 1, 0))
-        square(1, 0, 1, 2)
-        square(2, 1, 0, 2)
-        square(2, 0, 1, 2)
-        square(3, 0, 1, 2)
-        multiply((1, 1, 1), (1, 1, 0))
+        multiply((0, 1, 3), (0, 1, 2))
         copy_out(3, 1, 0, 2)
-        multiply((2, 0, 0), (2, 0, 1), (2, 1, 1))
-        square(1, 1, 1, 2)
-        add(0, 1, 1, 2)
-        square(0, 1, 1, 2)
-        multiply((2, 0, 2), (3, 0, 3), (2, 0, 3), (3, 1, 0))
-        add(0, 1, 2, 4)
-        square_copy(3, 1, 0, 2)
-        square(0, 0, 1, 3)
-        square(1, 0, 2, 4)
-        log(0, 1, 1, 4)
-        square(2, 0, 2, 3)
-        multiply((3, 1, 2))
-        add(0, 1, 0, 1)
-        copy_out(3, 1, 2, 3)
-        add(1, 2, 0, 4)
-        log(0, 1, 0, 1)
-        add(2, 3, 1, 2)
+        square(0, 1, 0, 1)
+        quantize_x(3, 4)
+        multiply((1, 1, 2))
+        square(0, 0, 1, 2)
+        multiply((1, 1, 1))
+        square(1, 0, 1, 2)
+        multiply((1, 1, 0), (2, 0, 0))
+        square(3, 0, 1, 2)
         multiply((2, 1, 0))
-        halve(0, 1, 0, 4)
-        square(0, 0, 3, 4)
-        multiply((3, 0, 0), (3, 0, 2), (3, 1, 1))
-        square_copy(3, 1, 2, 3)
-        square(0, 1, 2, 4)
-        store(0, 1, 0, 4)
-        log(1, 2, 0, 4)
-        multiply((2, 1, 2), (3, 0, 1))
-        add(2, 4, 0, 1)
+        add(0, 1, 3, 4)
+        square(2, 0, 1, 2)
+        multiply((2, 0, 1))
+        add(0, 1, 0, 3)
+        multiply((2, 0, 3))
+        square_copy(3, 1, 0, 2)
+        square(2, 1, 1, 2)
+        square(1, 1, 1, 2)
+        multiply((2, 1, 1))
+        square(0, 1, 1, 2)
+        log(0, 1, 3, 4)
         multiply((2, 1, 3))
-        copy_out(2, 0, 3, 4)
-        halve(1, 2, 0, 4)
-        store(1, 2, 0, 4)
+        square(0, 0, 2, 4)
+        copy_out(1, 0, 2, 3)
+        multiply((2, 0, 2))
+        log(0, 1, 0, 3)
+        multiply((3, 0, 1))
         square(3, 0, 2, 4)
-        square_copy(2, 0, 3, 4)
-        multiply((3, 1, 3))
-        square(3, 1, 3, 4)
-        log(2, 3, 0, 2)
-        add(2, 4, 3, 4)
-        log(3, 4, 0, 1)
+        multiply((2, 1, 2))
+        copy_out(1, 0, 3, 4)
+        multiply((3, 1, 3), (3, 1, 1))
+        square(2, 0, 2, 4)
+        add(1, 2, 0, 4)
+        halve(0, 1, 0, 4)
+        multiply((3, 0, 3))
+        store(0, 1, 0, 4)
+        add(2, 3, 0, 1)
+        multiply((3, 1, 2))
+        square_copy(1, 0, 2, 3)
+        square(3, 1, 2, 4)
+        log(1, 2, 0, 4)
+        multiply((3, 1, 0))
         square(1, 1, 2, 4)
-        halve(2, 3, 1, 2)
-        add(2, 3, 2, 3)
-        halve(2, 4, 0, 1)
+        square_copy(1, 0, 3, 4)
+        multiply((3, 0, 0), (3, 0, 2))
+        add(2, 4, 3, 4)
+        square(0, 1, 2, 4)
+        log(2, 4, 3, 4)
+        halve(1, 2, 0, 4)
+        log(2, 3, 0, 1)
+        add(2, 3, 1, 3)
         square(2, 1, 2, 4)
-        store(2, 3, 1, 2)
-        store(2, 4, 0, 1)
-        log(3, 4, 3, 4)
-        log(2, 3, 3, 4)
-        add(3, 4, 1, 2)
-        log(2, 3, 2, 3)
+        add(3, 4, 0, 2)
+        halve(2, 4, 3, 4)
+        log(2, 3, 1, 2)
         log(3, 4, 1, 2)
+        halve(2, 3, 0, 1)
+        store(1, 2, 0, 4)
+        store(2, 4, 3, 4)
+        log(3, 4, 0, 1)
         add(3, 4, 2, 3)
-        halve(3, 4, 3, 4)
-        log(3, 4, 2, 3)
-        halve(2, 3, 3, 4)
-        store(3, 4, 3, 4)
-        store(2, 3, 3, 4)
-        halve(2, 3, 2, 3)
-        store(2, 3, 2, 3)
+        halve(2, 3, 1, 2)
         halve(3, 4, 1, 2)
-        halve(3, 4, 2, 3)
+        log(2, 3, 2, 3)
+        store(2, 3, 0, 1)
+        halve(3, 4, 0, 1)
+        store(2, 3, 1, 2)
+        halve(2, 3, 2, 3)
         store(3, 4, 1, 2)
+        store(3, 4, 0, 1)
+        log(3, 4, 2, 3)
+        store(2, 3, 2, 3)
+        halve(3, 4, 2, 3)
         store(3, 4, 2, 3)

from contextlib import ExitStack

import concourse.mybir as mybir

G, D, M, N = 4, 128, 128, 512
FLOPS = 2 * 2 * G * D * M * N

F32 = mybir.dt.float32
BF16 = mybir.dt.bfloat16
I32 = mybir.dt.int32
U32 = mybir.dt.uint32
U8 = mybir.dt.uint8
FP8X4 = mybir.dt.float8_e4m3fn_x4
ACT = mybir.ActivationFunctionType
ALU = mybir.AluOpType

P = 128
PACK = 4
ROWS = D // PACK
W = 128
SPLIT = 80


def tile_rows_dft_logmag_kernel(tc, x, fc, fs, out):
    nc = tc.nc
    x_rows = x.rearrange("g (p j) n -> (g p) j n", j=PACK)
    out_rows = out.rearrange("g m n -> m g n")
    fc_rows = fc.rearrange("(p j) m -> p j m", j=PACK)
    fs_rows = fs.rearrange("(p j) m -> p j m", j=PACK)

    with ExitStack() as ctx:
        sb = ctx.enter_context(tc.tile_pool(name="sb", bufs=1))
        ps = ctx.enter_context(tc.psum_pool(name="ps", bufs=1))
        ctx.enter_context(tc.manual_schedule())

        warm = sb.tile([P, 2], F32, name="warm")
        f_raw = sb.tile([P, PACK, M], F32, name="f_raw")
        f_bf = sb.tile([P, M, PACK], BF16, name="f_bf", align_bytes=64)
        f_mx = [sb.tile([P, M + M // 4], U32, name="f_mx%d" % s, align_bytes=64) for s in range(2)]
        x_raw = {}
        x_bf = sb.tile([P, N, PACK], BF16, name="x_bf", align_bytes=64)
        x_codes = sb.tile([P, N], U32, name="x_codes", align_bytes=64)
        x_scales = sb.tile([P, N], U8, name="x_scales", align_bytes=64)
        sums = sb.tile([P, G, 2, 4, W], F32, name="sums")
        squares = sb.tile([P, G, 2, 4, W], F32, name="squares")
        power = sb.tile([P, G, N], F32, name="power")
        logp = sb.tile([P, G, N], F32, name="logp")
        result = sb.tile([P, G, N], F32, name="result")
        acc = [[ps.tile([P, 4, W], F32, name="acc%d_%d" % (g, b)) for b in range(2)] for g in range(G)]

        def rows(g):
            return slice(ROWS * g, ROWS * (g + 1))

        def cols(c0, c1):
            return slice(W * c0, W * c1)

        def load_basis(g, queue):
            queue.dma_start(out=f_raw[rows(g), :, :], in_=fc_rows if g < G // 2 else fs_rows)

        def load_x(c0, c1):
            raw = sb.tile([P, PACK, W * (c1 - c0)], F32, name="x_raw%d" % c0)
            for c in range(c0, c1):
                x_raw[c] = (raw, c0)
            nc.sync.dma_start(out=raw[:], in_=x_rows[:, :, cols(c0, c1)])

        def interleave(dst, src):
            nc.vector.tensor_copy(out=dst.rearrange("p (c i) j -> p c j i", i=4),
                                  in_=src.rearrange("p j (c i) -> p c j i", i=4))

        def interleave_scalar(dst, src):
            nc.scalar.copy(out=dst, in_=src.rearrange("p j w -> p w j"))

        def quantize(codes, scales, src):
            nc.vector.quantize_mx(out=codes.bitcast(FP8X4), scales=scales, in_=src.rearrange("p w j -> p (w j)"))

        def interleave_x(c0, c1):
            raw, first = x_raw[c0]
            interleave(x_bf[:, cols(c0, c1), :], raw[:, :, cols(c0 - first, c1 - first)])

        def quantize_x(c0, c1):
            quantize(x_codes[:, cols(c0, c1)], x_scales[:, cols(c0, c1)], x_bf[:, cols(c0, c1), :])

        def swap_halves():
            half = P // 2
            nc.scalar.dma_start(out=f_mx[1][half:, :].bitcast(I32), in_=f_mx[0][:half, :].bitcast(I32))
            nc.scalar.dma_start(out=f_mx[1][:half, :].bitcast(I32), in_=f_mx[0][half:, :].bitcast(I32))

        def multiply(*passes):
            for c, s, g in passes:
                nc.tensor.matmul_mx(
                    out=acc[g][c % 2][:, 2 * (c // 2) + s, :],
                    lhsT=f_mx[s][rows(g), :M].bitcast(FP8X4),
                    lhsT_scale=f_mx[s][rows(g), M:].bitcast(U8),
                    rhs=x_codes[rows(g), cols(c, c + 1)].bitcast(FP8X4),
                    rhs_scale=x_scales[rows(g), cols(c, c + 1)],
                    start=True, stop=True)

        def square(g, b, lo, hi):
            nc.scalar.activation(out=squares[:, g, b, lo:hi, :], in_=acc[g][b][:, lo:hi, :], func=ACT.Square)

        def copy_out(g, b, lo, hi):
            nc.vector.tensor_copy(out=sums[:, g, b, lo:hi, :], in_=acc[g][b][:, lo:hi, :])

        def square_copy(g, b, lo, hi):
            nc.vector.tensor_tensor(out=squares[:, g, b, lo:hi, :], in0=sums[:, g, b, lo:hi, :],
                                    in1=sums[:, g, b, lo:hi, :], op=ALU.mult)

        def add(c0, c1, g0, g1):
            banks = slice(c0 % 2, c0 % 2 + c1 - c0)
            place = 2 * (c0 // 2)
            nc.vector.scalar_tensor_tensor(
                out=power[:, g0:g1, cols(c0, c1)].rearrange("p g (c w) -> p g c w", w=W),
                in0=squares[:, g0:g1, banks, place, :], scalar=0.001, in1=squares[:, g0:g1, banks, place + 1, :],
                op0=ALU.add, op1=ALU.add)

        def log(c0, c1, g0, g1):
            nc.scalar.activation(out=logp[:, g0:g1, cols(c0, c1)], in_=power[:, g0:g1, cols(c0, c1)], func=ACT.Ln)

        def halve(c0, c1, g0, g1):
            nc.vector.tensor_scalar(out=result[:, g0:g1, cols(c0, c1)], in0=logp[:, g0:g1, cols(c0, c1)],
                                    scalar1=0.5, scalar2=None, op0=ALU.mult)

        def halve_scalar(c0, c1, g0, g1):
            nc.scalar.activation(out=result[:, g0:g1, cols(c0, c1)], in_=logp[:, g0:g1, cols(c0, c1)],
                                 func=ACT.Copy, scale=0.5)

        def store(c0, c1, g0, g1):
            nc.sync.dma_start(out=out_rows[:, g0:g1, cols(c0, c1)], in_=result[:, g0:g1, cols(c0, c1)])

        load_basis(0, nc.sync)
        load_basis(2, nc.scalar)
        load_basis(1, nc.sync)
        load_basis(3, nc.scalar)
        load_x(0, 1)
        nc.vector.memset(warm[:, 0:1], 1.0)
        nc.vector.memset(f_mx[0][:, M:], 0)
        nc.scalar.activation(out=warm[:, 1:2], in_=warm[:, 0:1], func=ACT.Ln)
        load_x(1, 2)
        load_x(2, 4)
        interleave(f_bf[:, :SPLIT, :], f_raw[:, :, :SPLIT])
        interleave_scalar(f_bf[:, SPLIT:, :], f_raw[:, :, SPLIT:])
        interleave_scalar(x_bf[:, W * 0 + SPLIT : W * 1, :], x_raw[0][0][:, :, SPLIT:])
        quantize(f_mx[0][:, :M], f_mx[0][:, M:].bitcast(U8), f_bf[:])
        swap_halves()
        interleave(x_bf[:, W * 0 : W * 0 + SPLIT, :], x_raw[0][0][:, :, :SPLIT])
        quantize_x(0, 1)
        interleave_scalar(x_bf[:, W * 1 + SPLIT : W * 2, :], x_raw[1][0][:, :, SPLIT:])
        multiply((0, 0, 2))
        interleave(x_bf[:, W * 1 : W * 1 + SPLIT, :], x_raw[1][0][:, :, :SPLIT])
        multiply((0, 0, 0))
        square(2, 0, 0, 1)
        multiply((0, 0, 1))
        quantize_x(1, 2)
        square(0, 0, 0, 1)
        multiply((0, 0, 3))
        interleave_x(2, 3)
        interleave_x(3, 4)
        multiply((1, 0, 2), (1, 0, 3), (1, 0, 1))
        quantize_x(2, 3)
        multiply((1, 0, 0))
        square(1, 0, 0, 1)
        multiply((0, 1, 0), (0, 1, 1))
        square(3, 0, 0, 1)
        square(2, 1, 0, 1)
        multiply((1, 1, 3))
        square(1, 1, 0, 1)
        multiply((0, 1, 3), (0, 1, 2))
        copy_out(3, 1, 0, 2)
        square(0, 1, 0, 1)
        quantize_x(3, 4)
        multiply((1, 1, 2))
        square(0, 0, 1, 2)
        multiply((1, 1, 1))
        square(1, 0, 1, 2)
        multiply((1, 1, 0), (2, 0, 0))
        square(3, 0, 1, 2)
        multiply((2, 1, 0))
        add(0, 1, 3, 4)
        square(2, 0, 1, 2)
        multiply((2, 0, 1))
        add(0, 1, 0, 3)
        multiply((2, 0, 3))
        square_copy(3, 1, 0, 2)
        square(2, 1, 1, 2)
        square(1, 1, 1, 2)
        multiply((2, 1, 1))
        square(0, 1, 1, 2)
        log(0, 1, 3, 4)
        multiply((2, 1, 3))
        square(0, 0, 2, 4)
        copy_out(1, 0, 2, 3)
        multiply((2, 0, 2))
        log(0, 1, 0, 3)
        multiply((3, 0, 1))
        square(3, 0, 2, 4)
        multiply((2, 1, 2))
        copy_out(1, 0, 3, 4)
        multiply((3, 1, 3), (3, 1, 1))
        square(2, 0, 2, 4)
        add(1, 2, 0, 4)
        halve(0, 1, 0, 4)
        multiply((3, 0, 3))
        store(0, 1, 0, 4)
        add(2, 3, 0, 1)
        multiply((3, 1, 2))
        square_copy(1, 0, 2, 3)
        square(3, 1, 2, 4)
        log(1, 2, 0, 4)
        multiply((3, 1, 0))
        square(1, 1, 2, 4)
        square_copy(1, 0, 3, 4)
        multiply((3, 0, 0), (3, 0, 2))
        add(2, 4, 3, 4)
        square(0, 1, 2, 4)
        log(2, 4, 3, 4)
        halve(1, 2, 0, 4)
        log(2, 3, 0, 1)
        add(2, 3, 1, 3)
        square(2, 1, 2, 4)
        add(3, 4, 0, 2)
        halve(2, 4, 3, 4)
        log(2, 3, 1, 2)
        log(3, 4, 1, 2)
        halve(2, 3, 0, 1)
        store(1, 2, 0, 4)
        store(2, 4, 3, 4)
        log(3, 4, 0, 1)
        add(3, 4, 2, 3)
        halve(2, 3, 1, 2)
        halve(3, 4, 1, 2)
        log(2, 3, 2, 3)
        store(2, 3, 0, 1)
        halve(3, 4, 0, 1)
        store(2, 3, 1, 2)
        halve(2, 3, 2, 3)
        store(3, 4, 1, 2)
        store(3, 4, 0, 1)
        log(3, 4, 2, 3)
        store(2, 3, 2, 3)
        halve(3, 4, 2, 3)
        store(3, 4, 2, 3)
